import numpy as np
import ml_dtypes


def mxq(x, axis, fmt="e4m3"):
    dtype, down = {"e4m3": (ml_dtypes.float8_e4m3fn, 7), "e5m2": (ml_dtypes.float8_e5m2, 14)}[fmt]
    v = np.moveaxis(np.asarray(x, np.float32).astype(ml_dtypes.bfloat16).astype(np.float64), axis, -1)
    blocks = v.reshape(v.shape[:-1] + (-1, 32))
    amax = np.abs(blocks).max(-1, keepdims=True)
    byte = np.maximum(np.where(amax > 0, np.frexp(amax)[1] - 1 + 127, 0) - down, 1)
    scale = np.exp2(byte - 127.0)
    codes = (blocks / scale).astype(np.float32).astype(dtype).astype(np.float64)
    return np.moveaxis((codes * scale).reshape(v.shape), -1, axis)


WIDE = False


def mx_kscale(k):
    if not WIDE:
        return np.ones(k)
    levels = np.array([10, -10, 5, -5, 0])
    if k % 512:
        return np.exp2(np.random.permutation(np.resize(levels, k // 32))).repeat(32)
    a = np.empty((k // 512, 16))
    for p in range(k // 512):
        a[p, :8] = np.random.permutation(np.resize(levels, 8))
        for g in range(8):
            far = levels[np.abs(levels - a[p, g]) >= 10]
            a[p, g + 8] = far[np.random.randint(len(far))]
    return np.exp2(a.ravel()).repeat(32)


def f64(x):
    return np.asarray(x).astype(np.float64)


def striped(idx):
    return np.tile(idx.reshape(-1, 16).T, (8, 1)).astype(np.uint16)


def unstriped(offs):
    return offs[:16].T.reshape(-1).astype(np.int64)


def pack_weight(w):
    k, n = w.shape
    w = f64(np.asarray(w, np.float32).astype(ml_dtypes.bfloat16)).reshape(k // 32, 32, n)
    amax = np.abs(w).max(1)
    byte = np.clip(np.where(amax > 0, np.frexp(amax)[1] - 1 + 127 - 7, 1), 1, 254)
    scaled = (w * np.exp2(127.0 - byte)[:, None, :]).reshape(k, n).astype(np.float32)
    words = np.ascontiguousarray(scaled.reshape(k // 512, 128, 4, n).transpose(0, 1, 3, 2)).astype(ml_dtypes.float8_e4m3fn).view(np.uint8)
    return words, np.ascontiguousarray(byte.astype(np.uint8).reshape(k // 512, 16, n))


def unpack_weight(words, scales):
    g, p, n, _ = words.shape
    vals = np.ascontiguousarray(words).view(ml_dtypes.float8_e4m3fn).astype(np.float64) * np.repeat(np.exp2(scales.astype(np.float64) - 127.0), 8, axis=1)[..., None]
    return vals.transpose(0, 1, 3, 2).reshape(g * 512, n)


def gelu(v):
    return 0.5 * v * (1.0 + np.tanh(np.sqrt(2.0 / np.pi) * (v + 0.044715 * v**3)))


K, T, E, C, N = 512, 512, 8, 128, 128


def by_expert(wq, xq):
    return np.concatenate([wq[e].T @ xq[:, e * C:(e + 1) * C] for e in range(E)], axis=1)


def setup_inputs():
    n = np.random.standard_normal
    s = mx_kscale(K)[:, None]
    first = np.random.permutation(np.repeat(np.arange(E), T // E))
    second = (first + 1 + np.random.permutation(np.repeat(np.arange(E - 1), -(-T // (E - 1)))[:T])) % E
    while np.bincount(second, minlength=E).max() != T // E:
        load = np.bincount(second, minlength=E); hi, lo = int(load.argmax()), int(load.argmin())
        t = np.flatnonzero((second == hi) & (first != lo))[0]; second[t] = lo
    slot_token = np.empty(E * C, np.int64); pos = np.empty((2, T), np.int64); fill = np.zeros(E, np.int64)
    place = np.stack([np.random.permutation(C) for _ in range(E)])
    for r, deal in enumerate((first, second)):
        for t in np.random.permutation(T):
            e = deal[t]; j = e * C + place[e, fill[e]]; fill[e] += 1; slot_token[j] = t; pos[r, t] = j
    g = np.random.uniform(0.2, 0.8, T)
    packed = [pack_weight(m) for m in n((E, K, N)) / np.sqrt(K) / s[None]]
    return {
        "xT": (n((K, T)) * s).astype(np.float32),
        "w_words": np.stack([m[0] for m in packed]),
        "w_scales": np.stack([m[1] for m in packed]),
        "b": (0.3 * n((N, E))).astype(np.float32),
        "gate": np.stack([np.tile(g, (N, 1)), np.tile(1.0 - g, (N, 1))]).astype(np.float32),
        "offs": striped(slot_token),
        "pos1": striped(pos[0]),
        "pos2": striped(pos[1]),
    }


def reference(xT, w_words, w_scales, b, gate, offs, pos1, pos2):
    idx = unstriped(offs)
    xq = mxq(f64(xT)[:, idx], 0, "e4m3")
    w = np.stack([unpack_weight(w_words[e], w_scales[e]) for e in range(E)])
    y = by_expert(w, xq)
    y = gelu(y + np.repeat(f64(b), C, axis=1))
    return f64(gate[0]) * y[:, unstriped(pos1)] + f64(gate[1]) * y[:, unstriped(pos2)]

from contextlib import ExitStack

import concourse.mybir as mybir

K, T, E, C, N = 512, 512, 8, 128, 128
P = 128
SLOTS = E * C
FLOPS = 2 * K * SLOTS * N

F32 = mybir.dt.float32
BF16 = mybir.dt.bfloat16
I32 = mybir.dt.int32
U32 = mybir.dt.uint32
U16 = mybir.dt.uint16
U8 = mybir.dt.uint8
FP8X4 = mybir.dt.float8_e4m3fn_x4
GELU = mybir.ActivationFunctionType.Gelu_apprx_tanh
MULT = mybir.AluOpType.mult

R = 4
CHUNKS = ((0, 256, 168, ((0, 256),)), (256, 384, 80, ((0, 128),)), (384, 512, 80, ((0, 128),)))
CODE_COLS = 1408
SCALE_COLS = 704
BYTE_CUTS = ((0, 512), (512, 768), (768, 896), (896, 1024))


def tile_routed_moe_kernel(tc, xT, w_words, w_scales, b, gate, offs, pos1, pos2, out):
    nc = tc.nc
    with ExitStack() as ctx:
        keep = ctx.enter_context(tc.tile_pool(name="keep", bufs=1))
        psum = ctx.enter_context(tc.psum_pool(name="psum", bufs=1))

        warm = keep.tile([P, 1], F32, name="warm")
        nc.vector.memset(warm[:], 0.0)
        nc.scalar.activation(warm[:], warm[:], GELU)

        x_rows = xT.rearrange("(p r) w -> p r w", r=R)
        raws = []
        for lo, hi, vec, quants in CHUNKS:
            raw = keep.tile([P, R, hi - lo], F32, name=f"raw{lo}")
            nc.sync.dma_start(raw[:], x_rows[:, :, lo:hi])
            raws.append(raw)

        offs_t = keep.tile([P, SLOTS // 16], U16, name="offs_t")
        nc.sync.dma_start(offs_t[:], offs)

        w_s = keep.tile([P, E * N], U8, name="w_s", align_bytes=64)
        nc.vector.memset(w_s[:].bitcast(I32), 0)
        for q in range(4):
            nc.sync.dma_start(
                w_s[32 * q : 32 * q + 4, :].bitcast(I32).rearrange("p (e n) -> p e n", e=E),
                w_scales[:, 0, 4 * q : 4 * q + 4, :].rearrange("e q n -> q e n").bitcast(I32),
            )
        w_c = keep.tile([P, E * N], U32, name="w_c", align_bytes=64)
        nc.sync.dma_start(
            w_c[:].bitcast(I32).rearrange("p (e n) -> p e n", e=E),
            w_words.rearrange("e a p n r -> p (e a) (n r)").bitcast(I32),
        )
        b_t = keep.tile([P, E], F32, name="b_t")
        nc.sync.dma_start(b_t[:], b)
        pos1_t = keep.tile([P, T // 16], U16, name="pos1_t")
        nc.sync.dma_start(pos1_t[:], pos1)
        pos2_t = keep.tile([P, T // 16], U16, name="pos2_t")
        nc.sync.dma_start(pos2_t[:], pos2)
        gates = keep.tile([P, 2, T], F32, name="gates")
        nc.sync.dma_start(gates[:], gate.rearrange("s p t -> p s t"))

        codes = keep.tile([P, CODE_COLS], U32, name="codes", align_bytes=64)
        scales = keep.tile([P, SCALE_COLS], U8, name="scales", align_bytes=64)
        nc.gpsimd.memset(scales[:], 0)
        nc.vector.memset(codes[:, T:].bitcast(I32), 0)

        for (lo, hi, vec, quants), raw in zip(CHUNKS, raws):
            grouped = keep.tile([P, hi - lo, R], BF16, name=f"grouped{lo}", align_bytes=64)
            for copy, u, v in ((nc.scalar.copy, vec, hi - lo), (nc.vector.tensor_copy, 0, vec)):
                copy(
                    grouped[:, u:v, :].rearrange("p (c i) r -> p c r i", i=4),
                    raw[:, :, u:v].rearrange("p r (c i) -> p c r i", i=4),
                )
            for u, v in quants:
                nc.vector.quantize_mx(
                    out=codes[:, lo + u : lo + v].bitcast(FP8X4),
                    scales=scales[:, lo + u : lo + v],
                    in_=grouped[:, u:v, :].rearrange("p w r -> p (w r)"),
                )

        slot_codes = keep.tile([P, SLOTS], U32, name="slot_codes", align_bytes=64)
        slot_scales = keep.tile([P, SLOTS], U8, name="slot_scales", align_bytes=64)
        nc.vector.tensor_copy(slot_codes[:], codes[:].indirect(offs_t[:]))
        for lo, hi in BYTE_CUTS:
            nc.vector.tensor_copy(slot_scales[:, lo:hi], scales[:].indirect(offs_t[:, lo // 16 : hi // 16]))

        y = keep.tile([P, SLOTS], F32, name="y")
        for e in range(E):
            cols = slice(e * C, (e + 1) * C)
            acc = psum.tile([N, C], F32, name=f"acc{e}")
            nc.tensor.matmul_mx(
                out=acc[:],
                lhsT=w_c[:, cols].bitcast(FP8X4),
                lhsT_scale=w_s[:, cols],
                rhs=slot_codes[:, cols].bitcast(FP8X4),
                rhs_scale=slot_scales[:, cols],
                start=True,
                stop=True,
            )
            nc.scalar.activation(y[:, cols], acc[:], GELU, bias=b_t[:, e : e + 1])

        first = keep.tile([P, T], F32, name="first")
        second = keep.tile([P, T], F32, name="second")
        total = keep.tile([P, T], F32, name="total")
        half = T // 2
        nc.vector.tensor_tensor(first[:], y[:].indirect(pos1_t[:]), gates[:, 0, :], MULT)
        for lo in (0, half):
            nc.vector.tensor_tensor(
                second[:, lo : lo + half],
                y[:].indirect(pos2_t[:, lo // 16 : (lo + half) // 16]),
                gates[:, 1, lo : lo + half],
                MULT,
            )
        for lo in (0, half):
            cols = slice(lo, lo + half)
            nc.vector.tensor_add(total[:, cols], first[:, cols], second[:, cols])
            nc.sync.dma_start(out[:, cols], total[:, cols])
